import numpy as np
import ml_dtypes


def mxq(x, axis, fmt="e4m3"):
    dtype, down = {"e4m3": (ml_dtypes.float8_e4m3fn, 7), "e5m2": (ml_dtypes.float8_e5m2, 14)}[fmt]
    v = np.moveaxis(np.asarray(x, np.float32).astype(ml_dtypes.bfloat16).astype(np.float64), axis, -1)
    blocks = v.reshape(v.shape[:-1] + (-1, 32))
    amax = np.abs(blocks).max(-1, keepdims=True)
    byte = np.maximum(np.where(amax > 0, np.frexp(amax)[1] - 1 + 127, 0) - down, 1)
    scale = np.exp2(byte - 127.0)
    codes = (blocks / scale).astype(np.float32).astype(dtype).astype(np.float64)
    return np.moveaxis((codes * scale).reshape(v.shape), -1, axis)


WIDE = False


def mx_kscale(k):
    if not WIDE:
        return np.ones(k)
    levels = np.array([10, -10, 5, -5, 0])
    if k % 512:
        return np.exp2(np.random.permutation(np.resize(levels, k // 32))).repeat(32)
    a = np.empty((k // 512, 16))
    for p in range(k // 512):
        a[p, :8] = np.random.permutation(np.resize(levels, 8))
        for g in range(8):
            far = levels[np.abs(levels - a[p, g]) >= 10]
            a[p, g + 8] = far[np.random.randint(len(far))]
    return np.exp2(a.ravel()).repeat(32)


def f64(x):
    return np.asarray(x).astype(np.float64)


def striped(idx):
    return np.tile(idx.reshape(-1, 16).T, (8, 1)).astype(np.uint16)


def unstriped(offs):
    return offs[:16].T.reshape(-1).astype(np.int64)


E2M1 = np.array([0.0, 0.5, 1.0, 1.5, 2.0, 3.0, 4.0, 6.0, -0.0, -0.5, -1.0, -1.5, -2.0, -3.0, -4.0, -6.0])


def pack_weight(w, fmt):
    k, n = w.shape
    w = f64(np.asarray(w, np.float32).astype(ml_dtypes.bfloat16)).reshape(k // 32, 32, n)
    amax = np.abs(w).max(1)
    if fmt == "e4m3":
        byte = np.frexp(amax)[1] - 1 + 127 - 7
    else:
        mant, ex = np.frexp(amax / 6.0)
        byte = np.where(mant > 0.5, ex, ex - 1) + 127
    byte = np.clip(np.where(amax > 0, byte, 1), 1, 254)
    scaled = (w * np.exp2(127.0 - byte)[:, None, :]).reshape(k, n).astype(np.float32)
    by_word = np.ascontiguousarray(scaled.reshape(k // 512, 128, 4, n).transpose(0, 1, 3, 2))
    if fmt == "e4m3":
        words = by_word.astype(ml_dtypes.float8_e4m3fn).view(np.uint8)
    else:
        c = by_word.astype(ml_dtypes.float4_e2m1fn).view(np.uint8) & 0xF
        words = (c[..., 0::2] | (c[..., 1::2] << 4)).reshape(k // 512, 128, 2 * n)
    return np.ascontiguousarray(words), np.ascontiguousarray(byte.astype(np.uint8).reshape(k // 512, 16, n))


def unpack_weight(words, scales, fmt):
    g, _, n = scales.shape
    words = np.ascontiguousarray(words).reshape(g, 128, n, -1)
    if fmt == "e4m3":
        vals = words.view(ml_dtypes.float8_e4m3fn).astype(np.float64)
    else:
        nib = np.empty((g, 128, n, 4), np.uint8)
        nib[..., 0::2] = words & 0xF
        nib[..., 1::2] = words >> 4
        vals = E2M1[nib]
    vals = vals * np.repeat(np.exp2(scales.astype(np.float64) - 127.0), 8, axis=1)[..., None]
    return vals.transpose(0, 1, 3, 2).reshape(g * 512, n)


def gelu(v):
    return 0.5 * v * (1.0 + np.tanh(np.sqrt(2.0 / np.pi) * (v + 0.044715 * v**3)))


def bf(x):
    return np.asarray(x, np.float32).astype(ml_dtypes.bfloat16)


def planes(Y):
    n, m = Y.shape
    b = f64(bf(Y)).reshape(n // 32, 32, m)
    amax = np.abs(b).max(1)
    byte = np.clip(np.where(amax > 0, np.frexp(amax)[1] - 1 + 127 - 7, 1), 1, 254)
    codes = (b * np.exp2(127.0 - byte)[:, None, :]).reshape(n, m).astype(np.float32).astype(ml_dtypes.float8_e4m3fn).view(np.uint8)
    words = codes.reshape(n // 512, 128, 4, m).transpose(0, 1, 3, 2)
    return np.ascontiguousarray(words), np.ascontiguousarray(byte.astype(np.uint8).reshape(n // 512, 16, m))


K, H, T, S, P = 1024, 512, 4096, 1024, 512

def setup_inputs():
    n = np.random.standard_normal
    s = mx_kscale(K)[:, None]
    u = mx_kscale(H)[:, None]
    d = {}
    d["tab_words"], d["tab_scales"] = pack_weight(n((K, T)) * s, "e4m3")
    d["offs"] = striped(np.random.permutation(T)[:S])
    d["pos1"] = striped(np.random.permutation(S)[:P])
    d["pos2"] = striped(np.random.permutation(S)[:P])
    d["w1"] = (0.8 * n((K, H)) / K**0.5 / s).astype(np.float32)
    d["w2_words"], d["w2_scales"] = pack_weight(n((K, H)) / K**0.5 / s, "e2m1")
    d["light"] = (0.8 * n((H, S))).astype(np.float32)
    d["gain"] = (np.exp(0.3 * n(H)) * u[:, 0]).astype(np.float32)
    d["w3"] = (1.2 * n((H, H)) / H**0.5 / u).astype(np.float32)
    d["tone"] = (0.5 * np.exp(0.8 * n(H))).astype(np.float32)
    return d

def reference(tab_words, tab_scales, offs, pos1, pos2, w1, w2_words, w2_scales, light, gain, w3, tone):
    v = unpack_weight(tab_words, tab_scales, "e4m3")[:, unstriped(offs)]
    w2 = unpack_weight(w2_words, w2_scales, "e2m1")
    base = mxq(f64(w1), 0, "e4m3").T @ v
    tint = w2.T @ v
    f = base + f64(light) * tint
    h = f * f64(gain)[:, None]
    t = mxq(f64(w3), 0, "e4m3").T @ mxq(h, 0, "e4m3")
    gelu = 0.5 * t * (1.0 + np.tanh(np.sqrt(2.0 / np.pi) * (t + 0.044715 * t**3)))
    g2 = gelu + f
    y = g2[:, unstriped(pos1)] * g2[:, unstriped(pos2)] * f64(tone)[:, None]
    words, scales = planes(y)
    return y, words, scales

@@ -1,0 +1,290 @@
+from contextlib import ExitStack
+
+import concourse.mybir as mybir
+
+K, H, T, S, M = 1024, 512, 4096, 1024, 512
+FLOPS = 2 * (2 * K * H * S + H * H * S)
+
+F32 = mybir.dt.float32
+BF16 = mybir.dt.bfloat16
+I32 = mybir.dt.int32
+U32 = mybir.dt.uint32
+U16 = mybir.dt.uint16
+U8 = mybir.dt.uint8
+FP8X4 = mybir.dt.float8_e4m3fn_x4
+FP4X4 = mybir.dt.float4_e2m1fn_x4
+MULT = mybir.AluOpType.mult
+ADD = mybir.AluOpType.add
+COPY = mybir.ActivationFunctionType.Copy
+GELU = mybir.ActivationFunctionType.Gelu_apprx_tanh
+
+P = 128
+PACK = 4
+KP = P * PACK
+PASSES = K // KP
+N = 512
+HALVES = S // N
+MC = 256
+QUADS = 4
+
+
+def tile_list_iris_ring_pairs_kernel(
+    tc, tab_words, tab_scales, offs, pos1, pos2, w1, w2_words, w2_scales, light, gain, w3, tone, out_0, out_1, out_2
+):
+    nc = tc.nc
+    with ExitStack() as ctx:
+        keep = ctx.enter_context(tc.tile_pool(name="keep", bufs=1))
+        psum = ctx.enter_context(tc.psum_pool(name="psum", bufs=8))
+
+        def tile(name, shape, dtype):
+            return keep.tile(shape, dtype, name=name, align_bytes=64)
+
+        offs_sb = keep.tile([P, S // 16], U16, name="offs_sb")
+        pos1_sb = keep.tile([P, M // 16], U16, name="pos1_sb")
+        pos2_sb = keep.tile([P, M // 16], U16, name="pos2_sb")
+        tab_sb = [tile("tab%d" % a, [P, T], I32) for a in range(PASSES)]
+        tabsc_sb = tile("tabsc", [P, T], U8)
+        v_words = [[tile("v%d_%d" % (a, h), [P, N], U32) for h in range(HALVES)] for a in range(PASSES)]
+        v_sc = tile("v_sc", [P, S], U8)
+        v_sc1 = tile("v_sc1", [P, S], U8)
+        w2w_raw = tile("w2w_raw", [P, PASSES, 2 * H], U8)
+        w2s_raw = tile("w2s_raw", [P, PASSES, H], U8)
+        w2w = tile("w2w", [P, PASSES, 2 * H], U8)
+        w2s = tile("w2s", [P, PASSES, H], U8)
+        gain_sb = tile("gain_sb", [P, PACK], F32)
+        tone_sb = tile("tone_sb", [P, PACK], F32)
+        tone_rows = tile("tone_rows", [P, PACK, MC], F32)
+        warm = tile("warm", [P, 2], F32)
+
+        nc.vector.memset(tabsc_sb[:].bitcast(I32), 0)
+        nc.vector.memset(w2s_raw[:].rearrange("p a c -> p (a c)").bitcast(I32), 0)
+        nc.vector.memset(v_sc1[:].bitcast(I32), 0)
+        nc.vector.memset(warm[:, 0:1], 0.0)
+        nc.scalar.activation(out=warm[:, 1:2], in_=warm[:, 0:1], func=GELU)
+
+        nc.sync.dma_start(offs_sb[:], offs)
+        for q in range(QUADS):
+            nc.scalar.dma_start(
+                out=tabsc_sb[32 * q : 32 * q + 8, :].bitcast(I32),
+                in_=tab_scales[:, 4 * q : 4 * q + 4, :].bitcast(I32),
+            )
+
+        def load_tab(a):
+            nc.sync.dma_start(out=tab_sb[a][:], in_=tab_words[a].rearrange("p n t -> p (n t)").bitcast(I32))
+
+        def load_weight(name, rows, parts):
+            width = H // parts
+            raws = []
+            for c in range(parts):
+                raw = tile("%s_raw%d" % (name, c), [P, PACK, width], F32)
+                nc.sync.dma_start(
+                    out=raw[:], in_=rows[:, c * width : (c + 1) * width].rearrange("(p j) n -> p j n", j=PACK)
+                )
+                raws.append(raw)
+            return raws
+
+        light_rows = light.rearrange("(p t) j -> p t j", t=PACK)
+
+        def load_light(h):
+            tiles = []
+            for u in range(2):
+                lt = tile("light%d_%d" % (h, u), [P, 2, N], F32)
+                nc.sync.dma_start(out=lt[:], in_=light_rows[:, 2 * u : 2 * u + 2, h * N : (h + 1) * N])
+                tiles.append(lt)
+            return tiles
+
+        load_tab(0)
+        nc.sync.dma_start(
+            out=w2w_raw[:].bitcast(I32), in_=w2_words.rearrange("a p c -> p a c").bitcast(I32)
+        )
+        w1_raw0 = load_weight("w1a", w1[0:KP, :], 1)
+        load_tab(1)
+        for q in range(QUADS):
+            nc.gpsimd.dma_start(
+                out=w2s_raw[32 * q : 32 * q + 4, :, :].bitcast(I32),
+                in_=w2_scales[:, 4 * q : 4 * q + 4, :].rearrange("a r c -> r a c").bitcast(I32),
+            )
+        nc.gpsimd.dma_start(out=gain_sb[:], in_=gain.rearrange("(p t) -> p t", t=PACK))
+        nc.gpsimd.dma_start(out=tone_sb[:], in_=tone.rearrange("(p t) -> p t", t=PACK))
+        light_sb = [load_light(0)]
+        w1_raw1 = load_weight("w1b", w1[KP : 2 * KP, :], 2)
+        light_sb.append(load_light(1))
+        w3_raw = load_weight("w3", w3, 1)
+        nc.sync.dma_start(pos1_sb[:], pos1)
+        nc.sync.dma_start(pos2_sb[:], pos2)
+
+        nc.vector.tensor_copy(out=v_sc[:], in_=tabsc_sb[:].indirect(offs_sb[:]))
+        for q in range(QUADS):
+            nc.scalar.dma_start(
+                out=v_sc1[32 * q : 32 * q + 4, :].bitcast(I32),
+                in_=v_sc[32 * q + 4 : 32 * q + 8, :].bitcast(I32),
+            )
+        v_scales = [v_sc, v_sc1]
+
+        def gather_words(a, h):
+            cols = N // 16
+            nc.vector.tensor_copy(
+                out=v_words[a][h][:],
+                in_=tab_sb[a][:].bitcast(U32).indirect(offs_sb[:, h * cols : (h + 1) * cols]),
+            )
+
+        for a in range(PASSES):
+            nc.vector.tensor_copy(
+                out=w2w[:, a, :].rearrange("p (t m b) -> p t m b", t=PACK, b=2),
+                in_=w2w_raw[:, a, :].rearrange("p (m t b) -> p t m b", t=PACK, b=2),
+            )
+        nc.vector.tensor_copy(
+            out=w2s[:].rearrange("p a (t m) -> p a t m", t=PACK),
+            in_=w2s_raw[:].rearrange("p a (m t) -> p a t m", t=PACK),
+        )
+        for h in range(HALVES):
+            gather_words(0, h)
+
+        for t in range(PACK):
+            nc.scalar.copy(out=tone_rows[:, t, :], in_=tone_sb[:, t : t + 1].to_broadcast([P, MC]))
+
+        def round_weight(name, raws, copiers):
+            grouped = tile(name + "_bf", [P, PACK, P, PACK], BF16)
+            mw = P // len(raws)
+            for c, raw in enumerate(raws):
+                copiers[c](
+                    out=grouped[:, :, c * mw : (c + 1) * mw, :].rearrange("p t m j -> p m j t"),
+                    in_=raw[:].rearrange("p j (m t) -> p m j t", t=PACK),
+                )
+            return grouped
+
+        def quantise(name, grouped, pieces):
+            width = grouped.shape[1] // PACK
+            codes = tile(name + "_codes", [P, width], U32)
+            scales = tile(name + "_scales", [P, width], U8)
+            step = width // pieces
+            for c in range(pieces):
+                cols = slice(c * step, (c + 1) * step)
+                nc.vector.quantize_mx(
+                    out=codes[:, cols].bitcast(FP8X4),
+                    scales=scales[:, cols],
+                    in_=grouped[:, PACK * c * step : PACK * (c + 1) * step],
+                )
+            return codes, scales
+
+        def flat(grouped):
+            return grouped[:].rearrange("p t m j -> p (t m j)")
+
+        w1_bf0 = round_weight("w1a", w1_raw0, [nc.scalar.copy])
+        w1_q = [quantise("w1a", flat(w1_bf0), 1)]
+        for h in range(HALVES):
+            gather_words(1, h)
+
+        f_sb = [[tile("f%d_%d" % (h, t), [P, N], F32) for t in range(PACK)] for h in range(HALVES)]
+
+        def tint_stage(h):
+            jc = slice(h * N, (h + 1) * N)
+            for t in range(PACK):
+                acc = psum.tile([P, N], F32, name="acc")
+                for a in range(PASSES):
+                    nc.tensor.matmul_mx(
+                        out=acc[:],
+                        lhsT=w2w[:, a, 2 * P * t : 2 * P * (t + 1)].bitcast(FP4X4),
+                        lhsT_scale=w2s[:, a, P * t : P * (t + 1)],
+                        rhs=v_words[a][h][:].bitcast(FP8X4),
+                        rhs_scale=v_scales[a][:, jc],
+                        start=(a == 0),
+                        stop=(a == PASSES - 1),
+                    )
+                nc.vector.tensor_tensor(
+                    out=f_sb[h][t][:], in0=acc[:], in1=light_sb[h][t // 2][:, t % 2, :], op=MULT
+                )
+
+        h_rows = [tile("h_rows%d" % h, [P, PACK, N], BF16) for h in range(HALVES)]
+
+        def base_stage(h):
+            jc = slice(h * N, (h + 1) * N)
+            for t in range(PACK):
+                mc = slice(P * t, P * (t + 1))
+                acc = psum.tile([P, N], F32, name="acc")
+                for a in range(PASSES):
+                    codes, scales = w1_q[a]
+                    nc.tensor.matmul_mx(
+                        out=acc[:],
+                        lhsT=codes[:, mc].bitcast(FP8X4),
+                        lhsT_scale=scales[:, mc],
+                        rhs=v_words[a][h][:].bitcast(FP8X4),
+                        rhs_scale=v_scales[a][:, jc],
+                        start=(a == 0),
+                        stop=(a == PASSES - 1),
+                    )
+                nc.vector.tensor_tensor(out=f_sb[h][t][:], in0=acc[:], in1=f_sb[h][t][:], op=ADD)
+                nc.scalar.activation(
+                    out=h_rows[h][:, t, :], in_=f_sb[h][t][:], func=COPY, scale=gain_sb[:, t : t + 1]
+                )
+
+        def weave(copier, name, rows):
+            width = rows.shape[2]
+            grouped = tile(name, [P, width * PACK], BF16)
+            copier(
+                out=grouped[:].rearrange("p (c i t) -> p c t i", i=4, t=PACK),
+                in_=rows.rearrange("p t (c i) -> p c t i", i=4),
+            )
+            return grouped
+
+        g2 = [tile("g2_%d" % t, [P, S], F32) for t in range(PACK)]
+
+        def second_stage(h, h_q, w3_q):
+            jc = slice(h * N, (h + 1) * N)
+            for t in range(PACK):
+                mc = slice(P * t, P * (t + 1))
+                acc = psum.tile([P, N], F32, name="acc")
+                nc.tensor.matmul_mx(
+                    out=acc[:],
+                    lhsT=w3_q[0][:, mc].bitcast(FP8X4),
+                    lhsT_scale=w3_q[1][:, mc],
+                    rhs=h_q[0][:].bitcast(FP8X4),
+                    rhs_scale=h_q[1][:],
+                    start=True,
+                    stop=True,
+                )
+                nc.scalar.activation(out=g2[t][:, jc], in_=acc[:], func=GELU)
+                nc.vector.tensor_tensor(out=g2[t][:, jc], in0=g2[t][:, jc], in1=f_sb[h][t][:], op=ADD)
+
+        tint_stage(0)
+        w1_bf1 = round_weight("w1b", w1_raw1, [nc.scalar.copy, nc.vector.tensor_copy])
+        w1_q.append(quantise("w1b", flat(w1_bf1), 2))
+        base_stage(0)
+        h_bf0 = weave(nc.scalar.copy, "h_bf0", h_rows[0][:])
+        w3_bf = round_weight("w3", w3_raw, [nc.scalar.copy])
+        tint_stage(1)
+        base_stage(1)
+        h_q0 = quantise("h0", h_bf0[:], 1)
+        w3_q = quantise("w3", flat(w3_bf), 1)
+        h_bf1 = weave(nc.vector.tensor_copy, "h_bf1", h_rows[1][:])
+        h_q1 = quantise("h1", h_bf1[:], 1)
+        second_stage(0, h_q0, w3_q)
+        second_stage(1, h_q1, w3_q)
+
+        y_rows = out_0.rearrange("(p t) m -> p t m", t=PACK)
+        words_out = out_1[0].rearrange("p m t -> p (m t)").bitcast(I32)
+        chunks = M // MC
+        for c in range(chunks):
+            oc = slice(c * (MC // 16), (c + 1) * (MC // 16))
+            mc = slice(c * MC, (c + 1) * MC)
+            left = tile("left%d" % c, [P, PACK, MC], F32)
+            y = tile("y%d" % c, [P, PACK, MC], F32)
+            for t in range(PACK):
+                nc.vector.tensor_tensor(
+                    out=left[:, t, :], in0=g2[t][:].indirect(pos1_sb[:, oc]), in1=tone_rows[:, t, :], op=MULT
+                )
+            for t in range(PACK):
+                nc.vector.tensor_tensor(
+                    out=y[:, t, :], in0=g2[t][:].indirect(pos2_sb[:, oc]), in1=left[:, t, :], op=MULT
+                )
+                if t % 2 == 1:
+                    nc.sync.dma_start(out=y_rows[:, t - 1 : t + 1, mc], in_=y[:, t - 1 : t + 1, :])
+            y_bf = weave(nc.scalar.copy if c < chunks - 1 else nc.vector.tensor_copy, "y_bf%d" % c, y[:])
+            codes, scales = quantise("y%d" % c, y_bf[:], 1)
+            nc.sync.dma_start(out=words_out[:, mc], in_=codes[:].bitcast(I32))
+            for q in range(QUADS):
+                queue = nc.scalar if q % 2 == 0 else nc.sync
+                queue.dma_start(
+                    out=out_2[0, 4 * q : 4 * q + 4, mc].bitcast(I32),
+                    in_=scales[32 * q : 32 * q + 4, :].bitcast(I32),
+                )

@@ -36,13 +36,12 @@ def tile_list_iris_ring_pairs_kernel(
         keep = ctx.enter_context(tc.tile_pool(name="keep", bufs=1))
         psum = ctx.enter_context(tc.psum_pool(name="psum", bufs=8))
 
-        def tile(name, shape, dtype):
-            return keep.tile(shape, dtype, name=name, align_bytes=64)
+        def tile(name, shape, dtype, tag=None):
+            return keep.tile(shape, dtype, name=name, tag=tag or name, align_bytes=64)
 
         offs_sb = keep.tile([P, S // 16], U16, name="offs_sb")
         pos1_sb = keep.tile([P, M // 16], U16, name="pos1_sb")
         pos2_sb = keep.tile([P, M // 16], U16, name="pos2_sb")
-        tab_sb = [tile("tab%d" % a, [P, T], I32) for a in range(PASSES)]
         tabsc_sb = tile("tabsc", [P, T], U8)
         v_words = [[tile("v%d_%d" % (a, h), [P, N], U32) for h in range(HALVES)] for a in range(PASSES)]
         v_sc = tile("v_sc", [P, S], U8)
@@ -62,42 +61,48 @@ def tile_list_iris_ring_pairs_kernel(
         nc.vector.memset(warm[:, 0:1], 0.0)
         nc.scalar.activation(out=warm[:, 1:2], in_=warm[:, 0:1], func=GELU)
 
-        nc.sync.dma_start(offs_sb[:], offs)
-        for q in range(QUADS):
-            nc.scalar.dma_start(
-                out=tabsc_sb[32 * q : 32 * q + 8, :].bitcast(I32),
-                in_=tab_scales[:, 4 * q : 4 * q + 4, :].bitcast(I32),
-            )
 
         def load_tab(a):
-            nc.sync.dma_start(out=tab_sb[a][:], in_=tab_words[a].rearrange("p n t -> p (n t)").bitcast(I32))
+            nc.sync.dma_start(out=tab_sb[:, a, :], in_=tab_words[a].rearrange("p n t -> p (n t)").bitcast(I32))
 
-        def load_weight(name, rows, parts):
+        def load_weight(name, rows, parts, tag):
             width = H // parts
-            raws = []
+            raw = tile(name + "_raw", [P, parts, PACK, width], F32, tag)
             for c in range(parts):
-                raw = tile("%s_raw%d" % (name, c), [P, PACK, width], F32)
                 nc.sync.dma_start(
-                    out=raw[:], in_=rows[:, c * width : (c + 1) * width].rearrange("(p j) n -> p j n", j=PACK)
+                    out=raw[:, c], in_=rows[:, c * width : (c + 1) * width].rearrange("(p j) n -> p j n", j=PACK)
                 )
-                raws.append(raw)
-            return raws
+            return [raw[:, c] for c in range(parts)]
 
         light_rows = light.rearrange("(p t) j -> p t j", t=PACK)
 
-        def load_light(h):
-            tiles = []
+        def load_light(h, tag):
+            lt = tile("light%d" % h, [P, PACK, N], F32, tag)
             for u in range(2):
-                lt = tile("light%d_%d" % (h, u), [P, 2, N], F32)
-                nc.sync.dma_start(out=lt[:], in_=light_rows[:, 2 * u : 2 * u + 2, h * N : (h + 1) * N])
-                tiles.append(lt)
-            return tiles
+                nc.sync.dma_start(
+                    out=lt[:, 2 * u : 2 * u + 2, :], in_=light_rows[:, 2 * u : 2 * u + 2, h * N : (h + 1) * N]
+                )
+            return lt
 
-        load_tab(0)
         nc.sync.dma_start(
             out=w2w_raw[:].bitcast(I32), in_=w2_words.rearrange("a p c -> p a c").bitcast(I32)
         )
-        w1_raw0 = load_weight("w1a", w1[0:KP, :], 1)
+        nc.sync.dma_start(offs_sb[:], offs)
+        w1_raw0 = load_weight("w1a", w1[0:KP, :], 1, "w1a_raw")
+        nc.sync.dma_start(pos1_sb[:], pos1)
+        nc.sync.dma_start(pos2_sb[:], pos2)
+        for q in range(QUADS):
+            nc.sync.dma_start(
+                out=tabsc_sb[32 * q : 32 * q + 8, :].bitcast(I32),
+                in_=tab_scales[:, 4 * q : 4 * q + 4, :].bitcast(I32),
+            )
+        for a in range(PASSES):
+            nc.vector.tensor_copy(
+                out=w2w[:, a, :].rearrange("p (t m b) -> p t m b", t=PACK, b=2),
+                in_=w2w_raw[:, a, :].rearrange("p (m t b) -> p t m b", t=PACK, b=2),
+            )
+        tab_sb = tile("tab", [P, PASSES, T], I32, "w2w_raw")
+        load_tab(0)
         load_tab(1)
         for q in range(QUADS):
             nc.gpsimd.dma_start(
@@ -106,12 +111,6 @@ def tile_list_iris_ring_pairs_kernel(
             )
         nc.gpsimd.dma_start(out=gain_sb[:], in_=gain.rearrange("(p t) -> p t", t=PACK))
         nc.gpsimd.dma_start(out=tone_sb[:], in_=tone.rearrange("(p t) -> p t", t=PACK))
-        light_sb = [load_light(0)]
-        w1_raw1 = load_weight("w1b", w1[KP : 2 * KP, :], 2)
-        light_sb.append(load_light(1))
-        w3_raw = load_weight("w3", w3, 1)
-        nc.sync.dma_start(pos1_sb[:], pos1)
-        nc.sync.dma_start(pos2_sb[:], pos2)
 
         nc.vector.tensor_copy(out=v_sc[:], in_=tabsc_sb[:].indirect(offs_sb[:]))
         for q in range(QUADS):
@@ -120,20 +119,16 @@ def tile_list_iris_ring_pairs_kernel(
                 in_=v_sc[32 * q + 4 : 32 * q + 8, :].bitcast(I32),
             )
         v_scales = [v_sc, v_sc1]
+        w1_raw1 = load_weight("w1b", w1[KP : 2 * KP, :], 2, "tabsc")
 
         def gather_words(a, h):
             cols = N // 16
             nc.vector.tensor_copy(
                 out=v_words[a][h][:],
-                in_=tab_sb[a][:].bitcast(U32).indirect(offs_sb[:, h * cols : (h + 1) * cols]),
+                in_=tab_sb[:, a, :].bitcast(U32).indirect(offs_sb[:, h * cols : (h + 1) * cols]),
             )
 
-        for a in range(PASSES):
-            nc.vector.tensor_copy(
-                out=w2w[:, a, :].rearrange("p (t m b) -> p t m b", t=PACK, b=2),
-                in_=w2w_raw[:, a, :].rearrange("p (m t b) -> p t m b", t=PACK, b=2),
-            )
-        nc.vector.tensor_copy(
+        nc.gpsimd.tensor_copy(
             out=w2s[:].rearrange("p a (t m) -> p a t m", t=PACK),
             in_=w2s_raw[:].rearrange("p a (m t) -> p a t m", t=PACK),
         )
@@ -149,7 +144,7 @@ def tile_list_iris_ring_pairs_kernel(
             for c, raw in enumerate(raws):
                 copiers[c](
                     out=grouped[:, :, c * mw : (c + 1) * mw, :].rearrange("p t m j -> p m j t"),
-                    in_=raw[:].rearrange("p j (m t) -> p m j t", t=PACK),
+                    in_=raw.rearrange("p j (m t) -> p m j t", t=PACK),
                 )
             return grouped
 
@@ -171,15 +166,17 @@ def tile_list_iris_ring_pairs_kernel(
             return grouped[:].rearrange("p t m j -> p (t m j)")
 
         w1_bf0 = round_weight("w1a", w1_raw0, [nc.scalar.copy])
+        light_sb = [load_light(0, "w1a_raw")]
         w1_q = [quantise("w1a", flat(w1_bf0), 1)]
         for h in range(HALVES):
             gather_words(1, h)
+        w3_raw = load_weight("w3", w3, 1, "w2w_raw")
 
         f_sb = [[tile("f%d_%d" % (h, t), [P, N], F32) for t in range(PACK)] for h in range(HALVES)]
 
-        def tint_stage(h):
+        def tint_stage(h, t):
             jc = slice(h * N, (h + 1) * N)
-            for t in range(PACK):
+            if True:
                 acc = psum.tile([P, N], F32, name="acc")
                 for a in range(PASSES):
                     nc.tensor.matmul_mx(
@@ -192,14 +189,14 @@ def tile_list_iris_ring_pairs_kernel(
                         stop=(a == PASSES - 1),
                     )
                 nc.vector.tensor_tensor(
-                    out=f_sb[h][t][:], in0=acc[:], in1=light_sb[h][t // 2][:, t % 2, :], op=MULT
+                    out=f_sb[h][t][:], in0=acc[:], in1=light_sb[h][:, t, :], op=MULT
                 )
 
         h_rows = [tile("h_rows%d" % h, [P, PACK, N], BF16) for h in range(HALVES)]
 
-        def base_stage(h):
+        def base_stage(h, t):
             jc = slice(h * N, (h + 1) * N)
-            for t in range(PACK):
+            if True:
                 mc = slice(P * t, P * (t + 1))
                 acc = psum.tile([P, N], F32, name="acc")
                 for a in range(PASSES):
@@ -246,16 +243,19 @@ def tile_list_iris_ring_pairs_kernel(
                 nc.scalar.activation(out=g2[t][:, jc], in_=acc[:], func=GELU)
                 nc.vector.tensor_tensor(out=g2[t][:, jc], in0=g2[t][:, jc], in1=f_sb[h][t][:], op=ADD)
 
-        tint_stage(0)
         w1_bf1 = round_weight("w1b", w1_raw1, [nc.scalar.copy, nc.vector.tensor_copy])
+        light_sb.append(load_light(1, "tabsc"))
         w1_q.append(quantise("w1b", flat(w1_bf1), 2))
-        base_stage(0)
+        for t in range(PACK):
+            tint_stage(0, t)
+            base_stage(0, t)
         h_bf0 = weave(nc.scalar.copy, "h_bf0", h_rows[0][:])
         w3_bf = round_weight("w3", w3_raw, [nc.scalar.copy])
-        tint_stage(1)
-        base_stage(1)
-        h_q0 = quantise("h0", h_bf0[:], 1)
         w3_q = quantise("w3", flat(w3_bf), 1)
+        h_q0 = quantise("h0", h_bf0[:], 1)
+        for t in range(PACK):
+            tint_stage(1, t)
+            base_stage(1, t)
         h_bf1 = weave(nc.vector.tensor_copy, "h_bf1", h_rows[1][:])
         h_q1 = quantise("h1", h_bf1[:], 1)
         second_stage(0, h_q0, w3_q)

@@ -24,7 +24,7 @@ KP = P * PACK
 PASSES = K // KP
 N = 512
 HALVES = S // N
-MC = 256
+CHUNKS = (384, 128)
 QUADS = 4
 
 
@@ -52,7 +52,6 @@ def tile_list_iris_ring_pairs_kernel(
         w2s = tile("w2s", [P, PASSES, H], U8)
         gain_sb = tile("gain_sb", [P, PACK], F32)
         tone_sb = tile("tone_sb", [P, PACK], F32)
-        tone_rows = tile("tone_rows", [P, PACK, MC], F32)
         warm = tile("warm", [P, 2], F32)
 
         nc.vector.memset(tabsc_sb[:].bitcast(I32), 0)
@@ -65,14 +64,10 @@ def tile_list_iris_ring_pairs_kernel(
         def load_tab(a):
             nc.sync.dma_start(out=tab_sb[:, a, :], in_=tab_words[a].rearrange("p n t -> p (n t)").bitcast(I32))
 
-        def load_weight(name, rows, parts, tag):
-            width = H // parts
-            raw = tile(name + "_raw", [P, parts, PACK, width], F32, tag)
-            for c in range(parts):
-                nc.sync.dma_start(
-                    out=raw[:, c], in_=rows[:, c * width : (c + 1) * width].rearrange("(p j) n -> p j n", j=PACK)
-                )
-            return [raw[:, c] for c in range(parts)]
+        def load_weight(name, rows, tag):
+            raw = tile(name + "_raw", [P, PACK, H], F32, tag)
+            nc.sync.dma_start(out=raw[:], in_=rows.rearrange("(p j) n -> p j n", j=PACK))
+            return raw
 
         light_rows = light.rearrange("(p t) j -> p t j", t=PACK)
 
@@ -88,7 +83,7 @@ def tile_list_iris_ring_pairs_kernel(
             out=w2w_raw[:].bitcast(I32), in_=w2_words.rearrange("a p c -> p a c").bitcast(I32)
         )
         nc.sync.dma_start(offs_sb[:], offs)
-        w1_raw0 = load_weight("w1a", w1[0:KP, :], 1, "w1a_raw")
+        w1_raw0 = load_weight("w1a", w1[0:KP, :], "w1a_raw")
         nc.sync.dma_start(pos1_sb[:], pos1)
         nc.sync.dma_start(pos2_sb[:], pos2)
         for q in range(QUADS):
@@ -96,11 +91,10 @@ def tile_list_iris_ring_pairs_kernel(
                 out=tabsc_sb[32 * q : 32 * q + 8, :].bitcast(I32),
                 in_=tab_scales[:, 4 * q : 4 * q + 4, :].bitcast(I32),
             )
-        for a in range(PASSES):
-            nc.vector.tensor_copy(
-                out=w2w[:, a, :].rearrange("p (t m b) -> p t m b", t=PACK, b=2),
-                in_=w2w_raw[:, a, :].rearrange("p (m t b) -> p t m b", t=PACK, b=2),
-            )
+        nc.vector.tensor_copy(
+            out=w2w[:].bitcast(U16).rearrange("p a (t m) -> p a t m", t=PACK),
+            in_=w2w_raw[:].bitcast(U16).rearrange("p a (m t) -> p a t m", t=PACK),
+        )
         tab_sb = tile("tab", [P, PASSES, T], I32, "w2w_raw")
         load_tab(0)
         load_tab(1)
@@ -119,7 +113,7 @@ def tile_list_iris_ring_pairs_kernel(
                 in_=v_sc[32 * q + 4 : 32 * q + 8, :].bitcast(I32),
             )
         v_scales = [v_sc, v_sc1]
-        w1_raw1 = load_weight("w1b", w1[KP : 2 * KP, :], 2, "tabsc")
+        w1_raw1 = load_weight("w1b", w1[KP : 2 * KP, :], "tabsc")
 
         def gather_words(a, h):
             cols = N // 16
@@ -135,42 +129,39 @@ def tile_list_iris_ring_pairs_kernel(
         for h in range(HALVES):
             gather_words(0, h)
 
-        for t in range(PACK):
-            nc.scalar.copy(out=tone_rows[:, t, :], in_=tone_sb[:, t : t + 1].to_broadcast([P, MC]))
-
-        def round_weight(name, raws, copiers):
+        def round_weight(name, raw, copiers):
             grouped = tile(name + "_bf", [P, PACK, P, PACK], BF16)
-            mw = P // len(raws)
-            for c, raw in enumerate(raws):
-                copiers[c](
-                    out=grouped[:, :, c * mw : (c + 1) * mw, :].rearrange("p t m j -> p m j t"),
-                    in_=raw.rearrange("p j (m t) -> p m j t", t=PACK),
+            share = PACK // len(copiers)
+            for c, copier in enumerate(copiers):
+                ts = slice(c * share, (c + 1) * share)
+                copier(
+                    out=grouped[:, ts].rearrange("p t m j -> p m t j"),
+                    in_=raw[:].rearrange("p j (m t) -> p m t j", t=PACK)[:, :, ts, :],
                 )
             return grouped
 
-        def quantise(name, grouped, pieces):
-            width = grouped.shape[1] // PACK
-            codes = tile(name + "_codes", [P, width], U32)
-            scales = tile(name + "_scales", [P, width], U8)
-            step = width // pieces
-            for c in range(pieces):
-                cols = slice(c * step, (c + 1) * step)
-                nc.vector.quantize_mx(
-                    out=codes[:, cols].bitcast(FP8X4),
-                    scales=scales[:, cols],
-                    in_=grouped[:, PACK * c * step : PACK * (c + 1) * step],
-                )
+        def quantise(name, grouped, widths):
+            codes = tile(name + "_codes", [P, sum(widths)], U32)
+            scales = tile(name + "_scales", [P, sum(widths)], U8)
+            first = 0
+            for width in widths:
+                quantise_into(codes, scales, first, grouped[:, PACK * first : PACK * (first + width)])
+                first = first + width
             return codes, scales
+
+        def quantise_into(codes, scales, first, grouped):
+            cols = slice(first, first + grouped.shape[1] // PACK)
+            nc.vector.quantize_mx(out=codes[:, cols].bitcast(FP8X4), scales=scales[:, cols], in_=grouped)
 
         def flat(grouped):
             return grouped[:].rearrange("p t m j -> p (t m j)")
 
         w1_bf0 = round_weight("w1a", w1_raw0, [nc.scalar.copy])
         light_sb = [load_light(0, "w1a_raw")]
-        w1_q = [quantise("w1a", flat(w1_bf0), 1)]
+        w1_q = [quantise("w1a", flat(w1_bf0), [H])]
         for h in range(HALVES):
             gather_words(1, h)
-        w3_raw = load_weight("w3", w3, 1, "w2w_raw")
+        w3_raw = load_weight("w3", w3, "w2w_raw")
 
         f_sb = [[tile("f%d_%d" % (h, t), [P, N], F32) for t in range(PACK)] for h in range(HALVES)]
 
@@ -215,6 +206,13 @@ def tile_list_iris_ring_pairs_kernel(
                     out=h_rows[h][:, t, :], in_=f_sb[h][t][:], func=COPY, scale=gain_sb[:, t : t + 1]
                 )
 
+        def first_stage(h):
+            tint_stage(h, 0)
+            for t in range(PACK):
+                if t + 1 < PACK:
+                    tint_stage(h, t + 1)
+                base_stage(h, t)
+
         def weave(copier, name, rows):
             width = rows.shape[2]
             grouped = tile(name, [P, width * PACK], BF16)
@@ -243,48 +241,54 @@ def tile_list_iris_ring_pairs_kernel(
                 nc.scalar.activation(out=g2[t][:, jc], in_=acc[:], func=GELU)
                 nc.vector.tensor_tensor(out=g2[t][:, jc], in0=g2[t][:, jc], in1=f_sb[h][t][:], op=ADD)
 
-        w1_bf1 = round_weight("w1b", w1_raw1, [nc.scalar.copy, nc.vector.tensor_copy])
+        w1_bf1 = round_weight("w1b", w1_raw1, [nc.vector.tensor_copy, nc.scalar.copy])
         light_sb.append(load_light(1, "tabsc"))
-        w1_q.append(quantise("w1b", flat(w1_bf1), 2))
-        for t in range(PACK):
-            tint_stage(0, t)
-            base_stage(0, t)
+        w1_q.append(quantise("w1b", flat(w1_bf1), [H // 2, H // 2]))
+        first_stage(0)
         h_bf0 = weave(nc.scalar.copy, "h_bf0", h_rows[0][:])
         w3_bf = round_weight("w3", w3_raw, [nc.scalar.copy])
-        w3_q = quantise("w3", flat(w3_bf), 1)
-        h_q0 = quantise("h0", h_bf0[:], 1)
-        for t in range(PACK):
-            tint_stage(1, t)
-            base_stage(1, t)
+        w3_q = quantise("w3", flat(w3_bf), [H])
+        h_q0 = quantise("h0", h_bf0[:], [N])
+        first_stage(1)
         h_bf1 = weave(nc.vector.tensor_copy, "h_bf1", h_rows[1][:])
-        h_q1 = quantise("h1", h_bf1[:], 1)
+        h_q1 = quantise("h1", h_bf1[:], [N])
         second_stage(0, h_q0, w3_q)
         second_stage(1, h_q1, w3_q)
 
         y_rows = out_0.rearrange("(p t) m -> p t m", t=PACK)
         words_out = out_1[0].rearrange("p m t -> p (m t)").bitcast(I32)
-        chunks = M // MC
-        for c in range(chunks):
-            oc = slice(c * (MC // 16), (c + 1) * (MC // 16))
-            mc = slice(c * MC, (c + 1) * MC)
-            left = tile("left%d" % c, [P, PACK, MC], F32)
-            y = tile("y%d" % c, [P, PACK, MC], F32)
+        y_codes = tile("y_codes", [P, M], U32)
+        y_scales = tile("y_scales", [P, M], U8)
+        first = 0
+        for c, width in enumerate(CHUNKS):
+            oc = slice(first // 16, (first + width) // 16)
+            mc = slice(first, first + width)
+            picked = tile("picked%d" % c, [P, PACK, width], F32)
+            toned = tile("toned%d" % c, [P, PACK, width], F32)
+            y = tile("y%d" % c, [P, PACK, width], F32)
             for t in range(PACK):
-                nc.vector.tensor_tensor(
-                    out=left[:, t, :], in0=g2[t][:].indirect(pos1_sb[:, oc]), in1=tone_rows[:, t, :], op=MULT
+                nc.vector.tensor_copy(out=picked[:, t, :], in_=g2[t][:].indirect(pos1_sb[:, oc]))
+                nc.scalar.activation(
+                    out=toned[:, t, :], in_=picked[:, t, :], func=COPY, scale=tone_sb[:, t : t + 1]
                 )
             for t in range(PACK):
                 nc.vector.tensor_tensor(
-                    out=y[:, t, :], in0=g2[t][:].indirect(pos2_sb[:, oc]), in1=left[:, t, :], op=MULT
+                    out=y[:, t, :], in0=g2[t][:].indirect(pos2_sb[:, oc]), in1=toned[:, t, :], op=MULT
                 )
                 if t % 2 == 1:
                     nc.sync.dma_start(out=y_rows[:, t - 1 : t + 1, mc], in_=y[:, t - 1 : t + 1, :])
-            y_bf = weave(nc.scalar.copy if c < chunks - 1 else nc.vector.tensor_copy, "y_bf%d" % c, y[:])
-            codes, scales = quantise("y%d" % c, y_bf[:], 1)
-            nc.sync.dma_start(out=words_out[:, mc], in_=codes[:].bitcast(I32))
-            for q in range(QUADS):
-                queue = nc.scalar if q % 2 == 0 else nc.sync
-                queue.dma_start(
-                    out=out_2[0, 4 * q : 4 * q + 4, mc].bitcast(I32),
-                    in_=scales[32 * q : 32 * q + 4, :].bitcast(I32),
-                )
+            last = c == len(CHUNKS) - 1
+            y_bf = weave(nc.vector.tensor_copy if last else nc.scalar.copy, "y_bf%d" % c, y[:])
+            done = 0
+            for piece in (256, 128):
+                if done + piece <= width:
+                    quantise_into(y_codes, y_scales, first + done, y_bf[:, PACK * done : PACK * (done + piece)])
+                    done = done + piece
+            nc.sync.dma_start(out=words_out[:, mc], in_=y_codes[:, mc].bitcast(I32))
+            first = first + width
+        for q in range(QUADS):
+            queue = nc.scalar if q % 2 == 0 else nc.sync
+            queue.dma_start(
+                out=out_2[0, 4 * q : 4 * q + 4, :].bitcast(I32),
+                in_=y_scales[32 * q : 32 * q + 4, :].bitcast(I32),
+            )

@@ -45,7 +45,7 @@ def tile_list_iris_ring_pairs_kernel(
         tabsc_sb = tile("tabsc", [P, T], U8)
         v_words = [[tile("v%d_%d" % (a, h), [P, N], U32) for h in range(HALVES)] for a in range(PASSES)]
         v_sc = tile("v_sc", [P, S], U8)
-        v_sc1 = tile("v_sc1", [P, S], U8)
+        v_planes = tile("v_planes", [P, PASSES, S], U8)
         w2w_raw = tile("w2w_raw", [P, PASSES, 2 * H], U8)
         w2s_raw = tile("w2s_raw", [P, PASSES, H], U8)
         w2w = tile("w2w", [P, PASSES, 2 * H], U8)
@@ -56,13 +56,15 @@ def tile_list_iris_ring_pairs_kernel(
 
         nc.vector.memset(tabsc_sb[:].bitcast(I32), 0)
         nc.vector.memset(w2s_raw[:].rearrange("p a c -> p (a c)").bitcast(I32), 0)
-        nc.vector.memset(v_sc1[:].bitcast(I32), 0)
+        nc.vector.memset(v_planes[:].rearrange("p a c -> p (a c)").bitcast(I32), 0)
         nc.vector.memset(warm[:, 0:1], 0.0)
         nc.scalar.activation(out=warm[:, 1:2], in_=warm[:, 0:1], func=GELU)
 
 
-        def load_tab(a):
-            nc.sync.dma_start(out=tab_sb[:, a, :], in_=tab_words[a].rearrange("p n t -> p (n t)").bitcast(I32))
+        def load_tab(a, tag):
+            words = tile("tab%d" % a, [P, T], I32, tag)
+            nc.sync.dma_start(out=words[:], in_=tab_words[a].rearrange("p n t -> p (n t)").bitcast(I32))
+            return words
 
         def load_weight(name, rows, tag):
             raw = tile(name + "_raw", [P, PACK, H], F32, tag)
@@ -83,23 +85,19 @@ def tile_list_iris_ring_pairs_kernel(
             out=w2w_raw[:].bitcast(I32), in_=w2_words.rearrange("a p c -> p a c").bitcast(I32)
         )
         nc.sync.dma_start(offs_sb[:], offs)
-        w1_raw0 = load_weight("w1a", w1[0:KP, :], "w1a_raw")
         nc.sync.dma_start(pos1_sb[:], pos1)
         nc.sync.dma_start(pos2_sb[:], pos2)
-        for q in range(QUADS):
-            nc.sync.dma_start(
-                out=tabsc_sb[32 * q : 32 * q + 8, :].bitcast(I32),
-                in_=tab_scales[:, 4 * q : 4 * q + 4, :].bitcast(I32),
-            )
+        nc.sync.dma_start(
+            out=tabsc_sb[0:P:4, :].bitcast(I32), in_=tab_scales.rearrange("a q c -> (a q) c").bitcast(I32)
+        )
+        w1_raw0 = load_weight("w1a", w1[0:KP, :], "w1a_raw")
         nc.vector.tensor_copy(
             out=w2w[:].bitcast(U16).rearrange("p a (t m) -> p a t m", t=PACK),
             in_=w2w_raw[:].bitcast(U16).rearrange("p a (m t) -> p a t m", t=PACK),
         )
-        tab_sb = tile("tab", [P, PASSES, T], I32, "w2w_raw")
-        load_tab(0)
-        load_tab(1)
+        tab_sb = [load_tab(0, "w2w_raw")]
         for q in range(QUADS):
-            nc.gpsimd.dma_start(
+            nc.scalar.dma_start(
                 out=w2s_raw[32 * q : 32 * q + 4, :, :].bitcast(I32),
                 in_=w2_scales[:, 4 * q : 4 * q + 4, :].rearrange("a r c -> r a c").bitcast(I32),
             )
@@ -107,27 +105,30 @@ def tile_list_iris_ring_pairs_kernel(
         nc.gpsimd.dma_start(out=tone_sb[:], in_=tone.rearrange("(p t) -> p t", t=PACK))
 
         nc.vector.tensor_copy(out=v_sc[:], in_=tabsc_sb[:].indirect(offs_sb[:]))
-        for q in range(QUADS):
-            nc.scalar.dma_start(
-                out=v_sc1[32 * q : 32 * q + 4, :].bitcast(I32),
-                in_=v_sc[32 * q + 4 : 32 * q + 8, :].bitcast(I32),
-            )
-        v_scales = [v_sc, v_sc1]
-        w1_raw1 = load_weight("w1b", w1[KP : 2 * KP, :], "tabsc")
+
+        def move_plane(a):
+            for q in range(QUADS):
+                row = 4 * (16 * a + 4 * q)
+                nc.sync.dma_start(
+                    out=v_planes[32 * q : 32 * q + 4, a, :].bitcast(I32),
+                    in_=v_sc[row : row + 16 : 4, :].bitcast(I32),
+                )
+
+        move_plane(0)
+        tab_sb.append(load_tab(1, "tabsc"))
+        move_plane(1)
 
         def gather_words(a, h):
             cols = N // 16
             nc.vector.tensor_copy(
                 out=v_words[a][h][:],
-                in_=tab_sb[:, a, :].bitcast(U32).indirect(offs_sb[:, h * cols : (h + 1) * cols]),
+                in_=tab_sb[a][:].bitcast(U32).indirect(offs_sb[:, h * cols : (h + 1) * cols]),
             )
 
-        nc.gpsimd.tensor_copy(
+        nc.vector.tensor_copy(
             out=w2s[:].rearrange("p a (t m) -> p a t m", t=PACK),
             in_=w2s_raw[:].rearrange("p a (m t) -> p a t m", t=PACK),
         )
-        for h in range(HALVES):
-            gather_words(0, h)
 
         def round_weight(name, raw, copiers):
             grouped = tile(name + "_bf", [P, PACK, P, PACK], BF16)
@@ -157,11 +158,15 @@ def tile_list_iris_ring_pairs_kernel(
             return grouped[:].rearrange("p t m j -> p (t m j)")
 
         w1_bf0 = round_weight("w1a", w1_raw0, [nc.scalar.copy])
-        light_sb = [load_light(0, "w1a_raw")]
+        w1_raw1 = load_weight("w1b", w1[KP : 2 * KP, :], "w1a_raw")
         w1_q = [quantise("w1a", flat(w1_bf0), [H])]
+        light_sb = [load_light(0, "w1a_bf")]
+        for h in range(HALVES):
+            gather_words(0, h)
+        w3_raw = load_weight("w3", w3, "w2w_raw")
         for h in range(HALVES):
             gather_words(1, h)
-        w3_raw = load_weight("w3", w3, "w2w_raw")
+        light_sb.append(load_light(1, "tabsc"))
 
         f_sb = [[tile("f%d_%d" % (h, t), [P, N], F32) for t in range(PACK)] for h in range(HALVES)]
 
@@ -175,7 +180,7 @@ def tile_list_iris_ring_pairs_kernel(
                         lhsT=w2w[:, a, 2 * P * t : 2 * P * (t + 1)].bitcast(FP4X4),
                         lhsT_scale=w2s[:, a, P * t : P * (t + 1)],
                         rhs=v_words[a][h][:].bitcast(FP8X4),
-                        rhs_scale=v_scales[a][:, jc],
+                        rhs_scale=v_planes[:, a, jc],
                         start=(a == 0),
                         stop=(a == PASSES - 1),
                     )
@@ -197,14 +202,20 @@ def tile_list_iris_ring_pairs_kernel(
                         lhsT=codes[:, mc].bitcast(FP8X4),
                         lhsT_scale=scales[:, mc],
                         rhs=v_words[a][h][:].bitcast(FP8X4),
-                        rhs_scale=v_scales[a][:, jc],
+                        rhs_scale=v_planes[:, a, jc],
                         start=(a == 0),
                         stop=(a == PASSES - 1),
                     )
                 nc.vector.tensor_tensor(out=f_sb[h][t][:], in0=acc[:], in1=f_sb[h][t][:], op=ADD)
-                nc.scalar.activation(
-                    out=h_rows[h][:, t, :], in_=f_sb[h][t][:], func=COPY, scale=gain_sb[:, t : t + 1]
-                )
+                if (h, t) == (HALVES - 1, PACK - 1):
+                    nc.scalar.activation(
+                        out=h_rows[h][:, t, :], in_=f_sb[h][t][:], func=COPY, scale=gain_sb[:, t : t + 1]
+                    )
+                else:
+                    nc.gpsimd.tensor_scalar(
+                        out=h_rows[h][:, t, :], in0=f_sb[h][t][:], scalar1=gain_sb[:, t : t + 1], scalar2=0.0,
+                        op0=MULT, op1=ADD,
+                    )
 
         def first_stage(h):
             tint_stage(h, 0)
@@ -224,9 +235,9 @@ def tile_list_iris_ring_pairs_kernel(
 
         g2 = [tile("g2_%d" % t, [P, S], F32) for t in range(PACK)]
 
-        def second_stage(h, h_q, w3_q):
+        def second_stage(h, t, h_q, w3_q):
             jc = slice(h * N, (h + 1) * N)
-            for t in range(PACK):
+            if True:
                 mc = slice(P * t, P * (t + 1))
                 acc = psum.tile([P, N], F32, name="acc")
                 nc.tensor.matmul_mx(
@@ -242,50 +253,59 @@ def tile_list_iris_ring_pairs_kernel(
                 nc.vector.tensor_tensor(out=g2[t][:, jc], in0=g2[t][:, jc], in1=f_sb[h][t][:], op=ADD)
 
         w1_bf1 = round_weight("w1b", w1_raw1, [nc.vector.tensor_copy, nc.scalar.copy])
-        light_sb.append(load_light(1, "tabsc"))
         w1_q.append(quantise("w1b", flat(w1_bf1), [H // 2, H // 2]))
         first_stage(0)
         h_bf0 = weave(nc.scalar.copy, "h_bf0", h_rows[0][:])
         w3_bf = round_weight("w3", w3_raw, [nc.scalar.copy])
+        first_stage(1)
         w3_q = quantise("w3", flat(w3_bf), [H])
         h_q0 = quantise("h0", h_bf0[:], [N])
-        first_stage(1)
         h_bf1 = weave(nc.vector.tensor_copy, "h_bf1", h_rows[1][:])
         h_q1 = quantise("h1", h_bf1[:], [N])
-        second_stage(0, h_q0, w3_q)
-        second_stage(1, h_q1, w3_q)
+        for t in range(PACK):
+            second_stage(0, t, h_q0, w3_q)
+
+        picked = tile("picked", [P, PACK, M], F32)
+        toned = tile("toned", [P, PACK, M], F32)
+        starts = [sum(CHUNKS[:c]) for c in range(len(CHUNKS))]
+
+        def pick_left(t):
+            nc.vector.tensor_copy(out=picked[:, t, :], in_=g2[t][:].indirect(pos1_sb[:]))
+            nc.scalar.activation(out=toned[:, t, :], in_=picked[:, t, :], func=COPY, scale=tone_sb[:, t : t + 1])
+
+        second_stage(1, 0, h_q1, w3_q)
+        for t in range(PACK):
+            if t + 1 < PACK:
+                second_stage(1, t + 1, h_q1, w3_q)
+            pick_left(t)
 
         y_rows = out_0.rearrange("(p t) m -> p t m", t=PACK)
         words_out = out_1[0].rearrange("p m t -> p (m t)").bitcast(I32)
         y_codes = tile("y_codes", [P, M], U32)
         y_scales = tile("y_scales", [P, M], U8)
-        first = 0
+        y_bf = []
         for c, width in enumerate(CHUNKS):
-            oc = slice(first // 16, (first + width) // 16)
-            mc = slice(first, first + width)
-            picked = tile("picked%d" % c, [P, PACK, width], F32)
-            toned = tile("toned%d" % c, [P, PACK, width], F32)
+            oc = slice(starts[c] // 16, (starts[c] + width) // 16)
+            mc = slice(starts[c], starts[c] + width)
             y = tile("y%d" % c, [P, PACK, width], F32)
             for t in range(PACK):
-                nc.vector.tensor_copy(out=picked[:, t, :], in_=g2[t][:].indirect(pos1_sb[:, oc]))
-                nc.scalar.activation(
-                    out=toned[:, t, :], in_=picked[:, t, :], func=COPY, scale=tone_sb[:, t : t + 1]
-                )
-            for t in range(PACK):
                 nc.vector.tensor_tensor(
-                    out=y[:, t, :], in0=g2[t][:].indirect(pos2_sb[:, oc]), in1=toned[:, t, :], op=MULT
+                    out=y[:, t, :], in0=g2[t][:].indirect(pos2_sb[:, oc]), in1=toned[:, t, mc], op=MULT
                 )
                 if t % 2 == 1:
                     nc.sync.dma_start(out=y_rows[:, t - 1 : t + 1, mc], in_=y[:, t - 1 : t + 1, :])
             last = c == len(CHUNKS) - 1
-            y_bf = weave(nc.vector.tensor_copy if last else nc.scalar.copy, "y_bf%d" % c, y[:])
+            y_bf.append(weave(nc.vector.tensor_copy if last else nc.scalar.copy, "y_bf%d" % c, y[:]))
+        for c, width in enumerate(CHUNKS):
+            mc = slice(starts[c], starts[c] + width)
             done = 0
             for piece in (256, 128):
                 if done + piece <= width:
-                    quantise_into(y_codes, y_scales, first + done, y_bf[:, PACK * done : PACK * (done + piece)])
+                    quantise_into(
+                        y_codes, y_scales, starts[c] + done, y_bf[c][:, PACK * done : PACK * (done + piece)]
+                    )
                     done = done + piece
             nc.sync.dma_start(out=words_out[:, mc], in_=y_codes[:, mc].bitcast(I32))
-            first = first + width
         for q in range(QUADS):
             queue = nc.scalar if q % 2 == 0 else nc.sync
             queue.dma_start(

from contextlib import ExitStack

import concourse.mybir as mybir

K, H, T, S, M = 1024, 512, 4096, 1024, 512
FLOPS = 2 * (2 * K * H * S + H * H * S)

F32 = mybir.dt.float32
BF16 = mybir.dt.bfloat16
I32 = mybir.dt.int32
U32 = mybir.dt.uint32
U16 = mybir.dt.uint16
U8 = mybir.dt.uint8
FP8X4 = mybir.dt.float8_e4m3fn_x4
FP4X4 = mybir.dt.float4_e2m1fn_x4
MULT = mybir.AluOpType.mult
ADD = mybir.AluOpType.add
COPY = mybir.ActivationFunctionType.Copy
GELU = mybir.ActivationFunctionType.Gelu_apprx_tanh

P = 128
PACK = 4
KP = P * PACK
PASSES = K // KP
N = 512
HALVES = S // N
CHUNKS = (384, 128)
QUADS = 4


def tile_list_iris_ring_pairs_kernel(
    tc, tab_words, tab_scales, offs, pos1, pos2, w1, w2_words, w2_scales, light, gain, w3, tone, out_0, out_1, out_2
):
    nc = tc.nc
    with ExitStack() as ctx:
        keep = ctx.enter_context(tc.tile_pool(name="keep", bufs=1))
        psum = ctx.enter_context(tc.psum_pool(name="psum", bufs=8))

        def tile(name, shape, dtype, tag=None):
            return keep.tile(shape, dtype, name=name, tag=tag or name, align_bytes=64)

        offs_sb = keep.tile([P, S // 16], U16, name="offs_sb")
        pos1_sb = keep.tile([P, M // 16], U16, name="pos1_sb")
        pos2_sb = keep.tile([P, M // 16], U16, name="pos2_sb")
        tabsc_sb = tile("tabsc", [P, T], U8)
        v_words = [[tile("v%d_%d" % (a, h), [P, N], U32) for h in range(HALVES)] for a in range(PASSES)]
        v_sc = tile("v_sc", [P, S], U8)
        v_planes = tile("v_planes", [P, PASSES, S], U8)
        w2w_raw = tile("w2w_raw", [P, PASSES, 2 * H], U8)
        w2s_raw = tile("w2s_raw", [P, PASSES, H], U8)
        w2w = tile("w2w", [P, PASSES, 2 * H], U8)
        w2s = tile("w2s", [P, PASSES, H], U8)
        gain_sb = tile("gain_sb", [P, PACK], F32)
        tone_sb = tile("tone_sb", [P, PACK], F32)
        warm = tile("warm", [P, 2], F32)

        nc.vector.memset(tabsc_sb[:].bitcast(I32), 0)
        nc.vector.memset(w2s_raw[:].rearrange("p a c -> p (a c)").bitcast(I32), 0)
        nc.vector.memset(v_planes[:].rearrange("p a c -> p (a c)").bitcast(I32), 0)
        nc.vector.memset(warm[:, 0:1], 0.0)
        nc.scalar.activation(out=warm[:, 1:2], in_=warm[:, 0:1], func=GELU)


        def load_tab(a, tag):
            words = tile("tab%d" % a, [P, T], I32, tag)
            nc.sync.dma_start(out=words[:], in_=tab_words[a].rearrange("p n t -> p (n t)").bitcast(I32))
            return words

        def load_weight(name, rows, tag):
            raw = tile(name + "_raw", [P, PACK, H], F32, tag)
            nc.sync.dma_start(out=raw[:], in_=rows.rearrange("(p j) n -> p j n", j=PACK))
            return raw

        light_rows = light.rearrange("(p t) j -> p t j", t=PACK)

        def load_light(h, tag):
            lt = tile("light%d" % h, [P, PACK, N], F32, tag)
            for u in range(2):
                nc.sync.dma_start(
                    out=lt[:, 2 * u : 2 * u + 2, :], in_=light_rows[:, 2 * u : 2 * u + 2, h * N : (h + 1) * N]
                )
            return lt

        nc.sync.dma_start(
            out=w2w_raw[:].bitcast(I32), in_=w2_words.rearrange("a p c -> p a c").bitcast(I32)
        )
        nc.sync.dma_start(offs_sb[:], offs)
        nc.sync.dma_start(pos1_sb[:], pos1)
        nc.sync.dma_start(pos2_sb[:], pos2)
        nc.sync.dma_start(
            out=tabsc_sb[0:P:4, :].bitcast(I32), in_=tab_scales.rearrange("a q c -> (a q) c").bitcast(I32)
        )
        w1_raw0 = load_weight("w1a", w1[0:KP, :], "w1a_raw")
        nc.vector.tensor_copy(
            out=w2w[:].bitcast(U16).rearrange("p a (t m) -> p a t m", t=PACK),
            in_=w2w_raw[:].bitcast(U16).rearrange("p a (m t) -> p a t m", t=PACK),
        )
        tab_sb = [load_tab(0, "w2w_raw")]
        for q in range(QUADS):
            nc.scalar.dma_start(
                out=w2s_raw[32 * q : 32 * q + 4, :, :].bitcast(I32),
                in_=w2_scales[:, 4 * q : 4 * q + 4, :].rearrange("a r c -> r a c").bitcast(I32),
            )
        nc.gpsimd.dma_start(out=gain_sb[:], in_=gain.rearrange("(p t) -> p t", t=PACK))
        nc.gpsimd.dma_start(out=tone_sb[:], in_=tone.rearrange("(p t) -> p t", t=PACK))

        nc.vector.tensor_copy(out=v_sc[:], in_=tabsc_sb[:].indirect(offs_sb[:]))

        def move_plane(a):
            for q in range(QUADS):
                row = 4 * (16 * a + 4 * q)
                nc.sync.dma_start(
                    out=v_planes[32 * q : 32 * q + 4, a, :].bitcast(I32),
                    in_=v_sc[row : row + 16 : 4, :].bitcast(I32),
                )

        move_plane(0)
        tab_sb.append(load_tab(1, "tabsc"))
        move_plane(1)

        def gather_words(a, h):
            cols = N // 16
            nc.vector.tensor_copy(
                out=v_words[a][h][:],
                in_=tab_sb[a][:].bitcast(U32).indirect(offs_sb[:, h * cols : (h + 1) * cols]),
            )

        nc.vector.tensor_copy(
            out=w2s[:].rearrange("p a (t m) -> p a t m", t=PACK),
            in_=w2s_raw[:].rearrange("p a (m t) -> p a t m", t=PACK),
        )

        def round_weight(name, raw, copiers):
            grouped = tile(name + "_bf", [P, PACK, P, PACK], BF16)
            share = PACK // len(copiers)
            for c, copier in enumerate(copiers):
                ts = slice(c * share, (c + 1) * share)
                copier(
                    out=grouped[:, ts].rearrange("p t m j -> p m t j"),
                    in_=raw[:].rearrange("p j (m t) -> p m t j", t=PACK)[:, :, ts, :],
                )
            return grouped

        def quantise(name, grouped, widths):
            codes = tile(name + "_codes", [P, sum(widths)], U32)
            scales = tile(name + "_scales", [P, sum(widths)], U8)
            first = 0
            for width in widths:
                quantise_into(codes, scales, first, grouped[:, PACK * first : PACK * (first + width)])
                first = first + width
            return codes, scales

        def quantise_into(codes, scales, first, grouped):
            cols = slice(first, first + grouped.shape[1] // PACK)
            nc.vector.quantize_mx(out=codes[:, cols].bitcast(FP8X4), scales=scales[:, cols], in_=grouped)

        def flat(grouped):
            return grouped[:].rearrange("p t m j -> p (t m j)")

        w1_bf0 = round_weight("w1a", w1_raw0, [nc.scalar.copy])
        w1_raw1 = load_weight("w1b", w1[KP : 2 * KP, :], "w1a_raw")
        w1_q = [quantise("w1a", flat(w1_bf0), [H])]
        light_sb = [load_light(0, "w1a_bf")]
        for h in range(HALVES):
            gather_words(0, h)
        w3_raw = load_weight("w3", w3, "w2w_raw")
        for h in range(HALVES):
            gather_words(1, h)
        light_sb.append(load_light(1, "tabsc"))

        f_sb = [[tile("f%d_%d" % (h, t), [P, N], F32) for t in range(PACK)] for h in range(HALVES)]

        def tint_stage(h, t):
            jc = slice(h * N, (h + 1) * N)
            if True:
                acc = psum.tile([P, N], F32, name="acc")
                for a in range(PASSES):
                    nc.tensor.matmul_mx(
                        out=acc[:],
                        lhsT=w2w[:, a, 2 * P * t : 2 * P * (t + 1)].bitcast(FP4X4),
                        lhsT_scale=w2s[:, a, P * t : P * (t + 1)],
                        rhs=v_words[a][h][:].bitcast(FP8X4),
                        rhs_scale=v_planes[:, a, jc],
                        start=(a == 0),
                        stop=(a == PASSES - 1),
                    )
                nc.vector.tensor_tensor(
                    out=f_sb[h][t][:], in0=acc[:], in1=light_sb[h][:, t, :], op=MULT
                )

        h_rows = [tile("h_rows%d" % h, [P, PACK, N], BF16) for h in range(HALVES)]

        def base_stage(h, t):
            jc = slice(h * N, (h + 1) * N)
            if True:
                mc = slice(P * t, P * (t + 1))
                acc = psum.tile([P, N], F32, name="acc")
                for a in range(PASSES):
                    codes, scales = w1_q[a]
                    nc.tensor.matmul_mx(
                        out=acc[:],
                        lhsT=codes[:, mc].bitcast(FP8X4),
                        lhsT_scale=scales[:, mc],
                        rhs=v_words[a][h][:].bitcast(FP8X4),
                        rhs_scale=v_planes[:, a, jc],
                        start=(a == 0),
                        stop=(a == PASSES - 1),
                    )
                nc.vector.tensor_tensor(out=f_sb[h][t][:], in0=acc[:], in1=f_sb[h][t][:], op=ADD)
                if (h, t) == (HALVES - 1, PACK - 1):
                    nc.scalar.activation(
                        out=h_rows[h][:, t, :], in_=f_sb[h][t][:], func=COPY, scale=gain_sb[:, t : t + 1]
                    )
                else:
                    nc.gpsimd.tensor_scalar(
                        out=h_rows[h][:, t, :], in0=f_sb[h][t][:], scalar1=gain_sb[:, t : t + 1], scalar2=0.0,
                        op0=MULT, op1=ADD,
                    )

        def first_stage(h):
            tint_stage(h, 0)
            for t in range(PACK):
                if t + 1 < PACK:
                    tint_stage(h, t + 1)
                base_stage(h, t)

        def weave(copier, name, rows):
            width = rows.shape[2]
            grouped = tile(name, [P, width * PACK], BF16)
            copier(
                out=grouped[:].rearrange("p (c i t) -> p c t i", i=4, t=PACK),
                in_=rows.rearrange("p t (c i) -> p c t i", i=4),
            )
            return grouped

        g2 = [tile("g2_%d" % t, [P, S], F32) for t in range(PACK)]

        def second_stage(h, t, h_q, w3_q):
            jc = slice(h * N, (h + 1) * N)
            if True:
                mc = slice(P * t, P * (t + 1))
                acc = psum.tile([P, N], F32, name="acc")
                nc.tensor.matmul_mx(
                    out=acc[:],
                    lhsT=w3_q[0][:, mc].bitcast(FP8X4),
                    lhsT_scale=w3_q[1][:, mc],
                    rhs=h_q[0][:].bitcast(FP8X4),
                    rhs_scale=h_q[1][:],
                    start=True,
                    stop=True,
                )
                nc.scalar.activation(out=g2[t][:, jc], in_=acc[:], func=GELU)
                nc.vector.tensor_tensor(out=g2[t][:, jc], in0=g2[t][:, jc], in1=f_sb[h][t][:], op=ADD)

        w1_bf1 = round_weight("w1b", w1_raw1, [nc.vector.tensor_copy, nc.scalar.copy])
        w1_q.append(quantise("w1b", flat(w1_bf1), [H // 2, H // 2]))
        first_stage(0)
        h_bf0 = weave(nc.scalar.copy, "h_bf0", h_rows[0][:])
        w3_bf = round_weight("w3", w3_raw, [nc.scalar.copy])
        first_stage(1)
        w3_q = quantise("w3", flat(w3_bf), [H])
        h_q0 = quantise("h0", h_bf0[:], [N])
        h_bf1 = weave(nc.vector.tensor_copy, "h_bf1", h_rows[1][:])
        h_q1 = quantise("h1", h_bf1[:], [N])
        for t in range(PACK):
            second_stage(0, t, h_q0, w3_q)

        picked = tile("picked", [P, PACK, M], F32)
        toned = tile("toned", [P, PACK, M], F32)
        starts = [sum(CHUNKS[:c]) for c in range(len(CHUNKS))]

        def pick_left(t):
            nc.vector.tensor_copy(out=picked[:, t, :], in_=g2[t][:].indirect(pos1_sb[:]))
            nc.scalar.activation(out=toned[:, t, :], in_=picked[:, t, :], func=COPY, scale=tone_sb[:, t : t + 1])

        second_stage(1, 0, h_q1, w3_q)
        for t in range(PACK):
            if t + 1 < PACK:
                second_stage(1, t + 1, h_q1, w3_q)
            pick_left(t)

        y_rows = out_0.rearrange("(p t) m -> p t m", t=PACK)
        words_out = out_1[0].rearrange("p m t -> p (m t)").bitcast(I32)
        y_codes = tile("y_codes", [P, M], U32)
        y_scales = tile("y_scales", [P, M], U8)
        y_bf = []
        for c, width in enumerate(CHUNKS):
            oc = slice(starts[c] // 16, (starts[c] + width) // 16)
            mc = slice(starts[c], starts[c] + width)
            y = tile("y%d" % c, [P, PACK, width], F32)
            for t in range(PACK):
                nc.vector.tensor_tensor(
                    out=y[:, t, :], in0=g2[t][:].indirect(pos2_sb[:, oc]), in1=toned[:, t, mc], op=MULT
                )
                if t % 2 == 1:
                    nc.sync.dma_start(out=y_rows[:, t - 1 : t + 1, mc], in_=y[:, t - 1 : t + 1, :])
            last = c == len(CHUNKS) - 1
            y_bf.append(weave(nc.vector.tensor_copy if last else nc.scalar.copy, "y_bf%d" % c, y[:]))
        for c, width in enumerate(CHUNKS):
            mc = slice(starts[c], starts[c] + width)
            done = 0
            for piece in (256, 128):
                if done + piece <= width:
                    quantise_into(
                        y_codes, y_scales, starts[c] + done, y_bf[c][:, PACK * done : PACK * (done + piece)]
                    )
                    done = done + piece
            nc.sync.dma_start(out=words_out[:, mc], in_=y_codes[:, mc].bitcast(I32))
        for q in range(QUADS):
            queue = nc.scalar if q % 2 == 0 else nc.sync
            queue.dma_start(
                out=out_2[0, 4 * q : 4 * q + 4, :].bitcast(I32),
                in_=y_scales[32 * q : 32 * q + 4, :].bitcast(I32),
            )
